import numpy as np
import ml_dtypes


def mxq(x, axis, fmt="e4m3"):
    dtype, down = {"e4m3": (ml_dtypes.float8_e4m3fn, 7), "e5m2": (ml_dtypes.float8_e5m2, 14)}[fmt]
    v = np.moveaxis(np.asarray(x, np.float32).astype(ml_dtypes.bfloat16).astype(np.float64), axis, -1)
    blocks = v.reshape(v.shape[:-1] + (-1, 32))
    amax = np.abs(blocks).max(-1, keepdims=True)
    byte = np.maximum(np.where(amax > 0, np.frexp(amax)[1] - 1 + 127, 0) - down, 1)
    scale = np.exp2(byte - 127.0)
    codes = (blocks / scale).astype(np.float32).astype(dtype).astype(np.float64)
    return np.moveaxis((codes * scale).reshape(v.shape), -1, axis)


WIDE = False


def mx_kscale(k):
    if not WIDE:
        return np.ones(k)
    levels = np.array([10, -10, 5, -5, 0])
    if k % 512:
        return np.exp2(np.random.permutation(np.resize(levels, k // 32))).repeat(32)
    a = np.empty((k // 512, 16))
    for p in range(k // 512):
        a[p, :8] = np.random.permutation(np.resize(levels, 8))
        for g in range(8):
            far = levels[np.abs(levels - a[p, g]) >= 10]
            a[p, g + 8] = far[np.random.randint(len(far))]
    return np.exp2(a.ravel()).repeat(32)


def f64(x):
    return np.asarray(x).astype(np.float64)


def striped(idx):
    return np.tile(np.asarray(idx).reshape(-1, 16).T, (8, 1)).astype(np.uint16)


def unstriped(offs):
    return offs[:16].T.reshape(-1).astype(np.int64)


def striped8(idx):
    return np.asarray(idx).reshape(8, -1, 16).transpose(0, 2, 1).reshape(128, -1).astype(np.uint16)


def unstriped8(offs):
    return offs.reshape(8, 16, -1).transpose(0, 2, 1).reshape(8, -1).astype(np.int64)


def pick8(x, idx, run):
    r = np.arange(len(x))
    return x[r[:, None], idx[r % (8 * run) // run]]


E2M1 = np.array([0.0, 0.5, 1.0, 1.5, 2.0, 3.0, 4.0, 6.0, -0.0, -0.5, -1.0, -1.5, -2.0, -3.0, -4.0, -6.0])


def pack_weight(w, fmt):
    k, n = w.shape
    w = f64(np.asarray(w, np.float32).astype(ml_dtypes.bfloat16)).reshape(k // 32, 32, n)
    amax = np.abs(w).max(1)
    if fmt == "e4m3":
        byte = np.frexp(amax)[1] - 1 + 127 - 7
    else:
        mant, ex = np.frexp(amax / 6.0)
        byte = np.where(mant > 0.5, ex, ex - 1) + 127
    byte = np.clip(np.where(amax > 0, byte, 1), 1, 254)
    scaled = (w * np.exp2(127.0 - byte)[:, None, :]).reshape(k, n).astype(np.float32)
    by_word = np.ascontiguousarray(scaled.reshape(k // 512, 128, 4, n).transpose(0, 1, 3, 2))
    if fmt == "e4m3":
        words = by_word.astype(ml_dtypes.float8_e4m3fn).view(np.uint8)
    else:
        c = by_word.astype(ml_dtypes.float4_e2m1fn).view(np.uint8) & 0xF
        words = (c[..., 0::2] | (c[..., 1::2] << 4)).reshape(k // 512, 128, 2 * n)
    return np.ascontiguousarray(words), np.ascontiguousarray(byte.astype(np.uint8).reshape(k // 512, 16, n))


def unpack_weight(words, scales, fmt):
    g, _, n = scales.shape
    words = np.ascontiguousarray(words).reshape(g, 128, n, -1)
    if fmt == "e4m3":
        vals = words.view(ml_dtypes.float8_e4m3fn).astype(np.float64)
    else:
        nib = np.empty((g, 128, n, 4), np.uint8)
        nib[..., 0::2] = words & 0xF
        nib[..., 1::2] = words >> 4
        vals = E2M1[nib]
    vals = vals * np.repeat(np.exp2(scales.astype(np.float64) - 127.0), 8, axis=1)[..., None]
    return vals.transpose(0, 1, 3, 2).reshape(g * 512, n)


def sgn(shape):
    return np.random.uniform(0.5, 2.0, shape) * np.where(np.random.standard_normal(shape) < 0, -1.0, 1.0)


K, J, R, T, F, G, O, N = 512, 256, 512, 512, 2048, 1024, 128, 256


def setup_inputs():
    n = np.random.standard_normal
    idx = np.random.permutation(T)[:J]
    idx2 = np.stack([np.random.permutation(F)[:R] for _ in range(8)])
    idx3 = np.stack([np.random.permutation(G)[:R] for _ in range(8)])
    idx4 = np.stack([np.random.permutation(G)[:R] for _ in range(8)])
    idx5 = np.stack([np.random.permutation(J)[:O] for _ in range(8)])
    idx6 = np.stack([np.random.permutation(J)[:O] for _ in range(8)])
    idx7 = np.stack([np.random.permutation(J)[:O] for _ in range(8)])
    fk = mx_kscale(K)
    fr = mx_kscale(R)
    xtp = pack_weight(n((K, T)) * fk[:, None], "e4m3")
    wbp = pack_weight(n((R, N)) * 1 / np.sqrt(R) / fr[:, None], "e4m3")
    return {
        "xt_words": xtp[0],
        "xt_scales": xtp[1],
        "ua": (np.random.randint(-7, 8, (K, F)).astype(np.float64)).astype(np.float32),
        "ha": ((np.random.randint(8, 25, (K, 1)) / 1024.0) / fk[:, None]).astype(np.float32),
        "hb": (np.random.uniform(0.5, 1.6, (K, 1))).astype(np.float32),
        "sa": (sgn((R, 1)) * fr[:, None]).astype(np.float32),
        "sb": (sgn((R, 1)) * fr[:, None]).astype(np.float32),
        "sd": (sgn((R, 1)) * fr[:, None]).astype(np.float32),
        "wb_words": wbp[0],
        "wb_scales": wbp[1],
        "offs": striped(idx),
        "offs2": striped8(idx2),
        "offs3": striped8(idx3),
        "offs4": striped8(idx4),
        "offs5": striped8(idx5),
        "offs6": striped8(idx6),
        "offs7": striped8(idx7),
    }


def reference(xt_words, xt_scales, ua, ha, hb, sa, sb, sd, wb_words, wb_scales, offs, offs2, offs3, offs4, offs5, offs6, offs7):
    idx = unstriped(offs)
    idx2 = unstriped8(offs2)
    idx3 = unstriped8(offs3)
    idx4 = unstriped8(offs4)
    idx5 = unstriped8(offs5)
    idx6 = unstriped8(offs6)
    idx7 = unstriped8(offs7)
    xtu = unpack_weight(xt_words, xt_scales, "e4m3")
    wbu = unpack_weight(wb_words, wb_scales, "e4m3")
    wcd = pick8(f64(ua), idx2, 64) * f64(ha)
    wcp = np.zeros((K, G))
    wcp[np.arange(K)[:, None], idx3[np.arange(K) % 512 // 64]] = wcd
    wc = pick8(wcp, idx4, 64) * f64(hb)
    wcq = mxq(wc, 0, "e4m3")
    xtidxg = xtu[:, idx]
    a = wcq.T @ xtidxg
    hid = np.maximum(pick8(a, idx5, 64) * f64(sa) + pick8(a, idx6, 64) * f64(sb) + pick8(a, idx7, 64) * f64(sd), 0.0)
    hidq = mxq(hid, 0, "e4m3")
    y = wbu.T @ hidq
    return y

@@ -1,0 +1,157 @@
+from contextlib import ExitStack
+
+import concourse.mybir as mybir
+
+K, J, R, T, F, G, O, N = 512, 256, 512, 512, 2048, 1024, 128, 256
+FLOPS = 2 * K * R * J + 2 * R * N * O
+
+F32 = mybir.dt.float32
+BF16 = mybir.dt.bfloat16
+I32 = mybir.dt.int32
+U32 = mybir.dt.uint32
+U16 = mybir.dt.uint16
+U8 = mybir.dt.uint8
+FP8X4 = mybir.dt.float8_e4m3fn_x4
+COPY = mybir.ActivationFunctionType.Copy
+ADD = mybir.AluOpType.add
+MAX = mybir.AluOpType.max
+
+P = 128
+PACK = 4
+HALF = R // 2
+
+
+def tile_picked_tokens_codepage_one_grouptriple_one_plain_kernel(
+    tc, xt_words, xt_scales, ua, ha, hb, sa, sb, sd, wb_words, wb_scales,
+    offs, offs2, offs3, offs4, offs5, offs6, offs7, out,
+):
+    nc = tc.nc
+    with ExitStack() as ctx:
+        lists = ctx.enter_context(tc.tile_pool(name="lists", bufs=1))
+        keep = ctx.enter_context(tc.tile_pool(name="keep", bufs=1))
+        psum = ctx.enter_context(tc.psum_pool(name="psum", bufs=1))
+
+        def load_list(src, name):
+            tile = lists.tile(list(src.shape), U16, name=name)
+            nc.sync.dma_start(tile[:], src)
+            return tile
+
+        def load_column(src, name, queue, tag):
+            tile = keep.tile([P, PACK], F32, name=name, tag=tag, align_bytes=64)
+            queue.dma_start(tile[:], src.rearrange("(p t) o -> p (t o)", t=PACK))
+            return tile
+
+        def load_scale_rows(plane, src):
+            for i in range(4):
+                nc.sync.dma_start(plane[i:P:32, :].bitcast(I32), src[0, i:16:4, :].bitcast(I32))
+
+        xs = keep.tile([P, T], U8, name="xs", align_bytes=64)
+        nc.vector.memset(xs[:].bitcast(I32), 0)
+        wbs = keep.tile([P, N], U8, name="wbs", align_bytes=64)
+        nc.gpsimd.memset(wbs[:], 0)
+        page = [keep.tile([P, G], F32, name="page%d" % t) for t in range(PACK)]
+        for t in range(PACK):
+            nc.vector.memset(page[t][:], 0.0)
+
+        ua_rows = ua.rearrange("(p t) f -> p t f", t=PACK)
+        table = [keep.tile([P, F], F32, name="table%d" % t) for t in range(PACK)]
+
+        list2 = load_list(offs2, "list2")
+        step = load_column(ha, "step", nc.scalar, "step_then_planes")
+        nc.sync.dma_start(table[0][:], ua_rows[:, 0, :])
+        load_scale_rows(xs, xt_scales)
+        list1 = load_list(offs, "list1")
+        list3 = load_list(offs3, "list3")
+        for t in range(1, PACK):
+            nc.sync.dma_start(table[t][:], ua_rows[:, t, :])
+        list4 = load_list(offs4, "list4")
+        reading = load_column(hb, "reading", nc.sync, "reading")
+        xw = keep.tile([P, T], I32, name="xw", align_bytes=64)
+        nc.sync.dma_start(xw[:], xt_words[0].rearrange("p c b -> p (c b)").bitcast(I32))
+        slot_lists = [load_list(src, "list%d" % (5 + i)) for i, src in enumerate((offs5, offs6, offs7))]
+        weights = [load_column(src, "weight%d" % i, nc.sync, "weight%d" % i) for i, src in enumerate((sa, sb, sd))]
+        wbw = keep.tile([P, N], I32, name="wbw", align_bytes=64)
+        nc.sync.dma_start(wbw[:], wb_words[0].rearrange("p c b -> p (c b)").bitcast(I32))
+        load_scale_rows(wbs, wb_scales)
+
+        xs_g = keep.tile([P, J], U8, name="xs_g", align_bytes=64)
+        nc.vector.tensor_copy(xs_g[:], xs[:].indirect(list1[:]))
+
+        for t in range(PACK):
+            wcd = keep.tile([P, R], F32, name="wcd%d" % t, tag="wcd%d" % t, align_bytes=64)
+            nc.scalar.activation(wcd[:], table[t][:].indirect(list2[:]), COPY, scale=step[:, t : t + 1])
+            nc.vector.tensor_copy(page[t][:].indirect(list3[:]), wcd[:])
+
+        xw_g = keep.tile([P, J], U32, name="xw_g", tag="wcd%d" % (PACK - 1), align_bytes=64)
+        nc.vector.tensor_copy(xw_g[:], xw[:].bitcast(U32).indirect(list1[:]))
+
+        planes = keep.tile([P, 2, PACK, HALF], BF16, name="planes", tag="step_then_planes", align_bytes=64)
+        for j in range(PACK):
+            for h in range(2):
+                cols = slice(h * HALF // 16, (h + 1) * HALF // 16)
+                nc.scalar.activation(
+                    planes[:, h, j, :], page[j][:].indirect(list4[:, cols]), COPY, scale=reading[:, j : j + 1]
+                )
+
+        grouped = [keep.tile([P, P, PACK], BF16, name="grouped%d" % t, align_bytes=64) for t in range(PACK)]
+
+        def interleave(h, t):
+            src = planes[:, h].rearrange("p j (m t) -> p t m j", t=PACK)
+            nc.vector.tensor_copy(grouped[t][:, h * 64 : (h + 1) * 64, :], src[:, t])
+
+        for t in range(PACK):
+            interleave(0, t)
+        banks = []
+        interleave(1, 0)
+        for t in range(PACK):
+            if t + 1 < PACK:
+                interleave(1, t + 1)
+            codes = keep.tile([P, P], U32, name="codes%d" % t, align_bytes=64)
+            scales = keep.tile([P, P], U8, name="scales%d" % t, align_bytes=64)
+            nc.vector.quantize_mx(
+                out=codes[:].bitcast(FP8X4), scales=scales[:], in_=grouped[t][:].rearrange("p m j -> p (m j)")
+            )
+            bank = psum.tile([P, J], F32, name="hidden_bank%d" % t)
+            nc.tensor.matmul_mx(
+                out=bank[:], lhsT=codes[:].bitcast(FP8X4), lhsT_scale=scales[:],
+                rhs=xw_g[:].bitcast(FP8X4), rhs_scale=xs_g[:], start=True, stop=True,
+            )
+            banks.append(bank)
+
+        hidden = [keep.tile([P, J], F32, name="hidden%d" % t) for t in range(PACK)]
+        nc.scalar.copy(hidden[0][:], banks[0][:])
+        for t in range(1, PACK):
+            nc.vector.tensor_copy(hidden[t][:], banks[t][:])
+
+        total = keep.tile([P, PACK, O], F32, name="total")
+        for t in range(PACK):
+            terms = [keep.tile([P, O], F32, name="term%d_%d" % (t, i)) for i in range(3)]
+            for i in range(3):
+                nc.scalar.activation(
+                    terms[i][:], hidden[t][:].indirect(slot_lists[i][:]), COPY, scale=weights[i][:, t : t + 1]
+                )
+            pair = keep.tile([P, O], F32, name="pair%d" % t)
+            nc.vector.tensor_tensor(pair[:], terms[0][:], terms[1][:], ADD)
+            nc.vector.tensor_tensor(total[:, t, :], pair[:], terms[2][:], ADD)
+
+        hid = keep.tile([P, O, PACK], BF16, name="hid", align_bytes=64)
+        nc.vector.tensor_scalar(hid[:], total[:].rearrange("p t o -> p o t"), 0.0, None, MAX)
+        hid_codes = keep.tile([P, O], U32, name="hid_codes", align_bytes=64)
+        hid_scales = keep.tile([P, O], U8, name="hid_scales", align_bytes=64)
+        nc.vector.quantize_mx(
+            out=hid_codes[:].bitcast(FP8X4), scales=hid_scales[:], in_=hid[:].rearrange("p o t -> p (o t)")
+        )
+        for h in range(N // P):
+            cols = slice(h * P, (h + 1) * P)
+            bank = psum.tile([P, O], F32, name="out_bank%d" % h)
+            nc.tensor.matmul_mx(
+                out=bank[:], lhsT=wbw[:, cols].bitcast(FP8X4), lhsT_scale=wbs[:, cols],
+                rhs=hid_codes[:].bitcast(FP8X4), rhs_scale=hid_scales[:], start=True, stop=True,
+            )
+            result = keep.tile([P, O], F32, name="result%d" % h)
+            if h == 0:
+                nc.scalar.copy(result[:], bank[:])
+                nc.scalar.dma_start(out[cols, :], result[:])
+            else:
+                nc.vector.tensor_copy(result[:], bank[:])
+                nc.sync.dma_start(out[cols, :], result[:])

@@ -45,6 +45,10 @@ def tile_picked_tokens_codepage_one_grouptriple_one_plain_kernel(
             for i in range(4):
                 nc.sync.dma_start(plane[i:P:32, :].bitcast(I32), src[0, i:16:4, :].bitcast(I32))
 
+        warm = keep.tile([P, 2], F32, name="warm")
+        nc.gpsimd.memset(warm[:, 0:1], 0.0)
+        nc.scalar.activation(warm[:, 1:2], warm[:, 0:1], COPY)
+
         xs = keep.tile([P, T], U8, name="xs", align_bytes=64)
         nc.vector.memset(xs[:].bitcast(I32), 0)
         wbs = keep.tile([P, N], U8, name="wbs", align_bytes=64)

@@ -29,6 +29,7 @@ def tile_picked_tokens_codepage_one_grouptriple_one_plain_kernel(
     with ExitStack() as ctx:
         lists = ctx.enter_context(tc.tile_pool(name="lists", bufs=1))
         keep = ctx.enter_context(tc.tile_pool(name="keep", bufs=1))
+        shared = ctx.enter_context(tc.tile_pool(name="shared", bufs=1))
         psum = ctx.enter_context(tc.psum_pool(name="psum", bufs=1))
 
         def load_list(src, name):
@@ -46,13 +47,13 @@ def tile_picked_tokens_codepage_one_grouptriple_one_plain_kernel(
                 nc.sync.dma_start(plane[i:P:32, :].bitcast(I32), src[0, i:16:4, :].bitcast(I32))
 
         warm = keep.tile([P, 2], F32, name="warm")
-        nc.gpsimd.memset(warm[:, 0:1], 0.0)
+        nc.vector.memset(warm[:, 0:1], 0.0)
         nc.scalar.activation(warm[:, 1:2], warm[:, 0:1], COPY)
 
         xs = keep.tile([P, T], U8, name="xs", align_bytes=64)
         nc.vector.memset(xs[:].bitcast(I32), 0)
         wbs = keep.tile([P, N], U8, name="wbs", align_bytes=64)
-        nc.gpsimd.memset(wbs[:], 0)
+        nc.vector.memset(wbs[:].bitcast(I32), 0)
         page = [keep.tile([P, G], F32, name="page%d" % t) for t in range(PACK)]
         for t in range(PACK):
             nc.vector.memset(page[t][:], 0.0)
@@ -63,31 +64,31 @@ def tile_picked_tokens_codepage_one_grouptriple_one_plain_kernel(
         list2 = load_list(offs2, "list2")
         step = load_column(ha, "step", nc.scalar, "step_then_planes")
         nc.sync.dma_start(table[0][:], ua_rows[:, 0, :])
-        load_scale_rows(xs, xt_scales)
-        list1 = load_list(offs, "list1")
         list3 = load_list(offs3, "list3")
-        for t in range(1, PACK):
+        for t in range(1, PACK - 1):
             nc.sync.dma_start(table[t][:], ua_rows[:, t, :])
-        list4 = load_list(offs4, "list4")
-        reading = load_column(hb, "reading", nc.sync, "reading")
+        list1 = load_list(offs, "list1")
         xw = keep.tile([P, T], I32, name="xw", align_bytes=64)
         nc.sync.dma_start(xw[:], xt_words[0].rearrange("p c b -> p (c b)").bitcast(I32))
+        load_scale_rows(xs, xt_scales)
+        nc.sync.dma_start(table[PACK - 1][:], ua_rows[:, PACK - 1, :])
+        list4 = load_list(offs4, "list4")
+        reading = load_column(hb, "reading", nc.sync, "reading")
         slot_lists = [load_list(src, "list%d" % (5 + i)) for i, src in enumerate((offs5, offs6, offs7))]
         weights = [load_column(src, "weight%d" % i, nc.sync, "weight%d" % i) for i, src in enumerate((sa, sb, sd))]
         wbw = keep.tile([P, N], I32, name="wbw", align_bytes=64)
         nc.sync.dma_start(wbw[:], wb_words[0].rearrange("p c b -> p (c b)").bitcast(I32))
         load_scale_rows(wbs, wb_scales)
 
-        xs_g = keep.tile([P, J], U8, name="xs_g", align_bytes=64)
-        nc.vector.tensor_copy(xs_g[:], xs[:].indirect(list1[:]))
-
         for t in range(PACK):
-            wcd = keep.tile([P, R], F32, name="wcd%d" % t, tag="wcd%d" % t, align_bytes=64)
+            wcd = shared.tile([P, R], F32, name="wcd%d" % t, align_bytes=64, offset=4 * R * (PACK - 1 - t))
             nc.scalar.activation(wcd[:], table[t][:].indirect(list2[:]), COPY, scale=step[:, t : t + 1])
             nc.vector.tensor_copy(page[t][:].indirect(list3[:]), wcd[:])
 
-        xw_g = keep.tile([P, J], U32, name="xw_g", tag="wcd%d" % (PACK - 1), align_bytes=64)
+        xw_g = shared.tile([P, J], U32, name="xw_g", align_bytes=64, offset=0)
         nc.vector.tensor_copy(xw_g[:], xw[:].bitcast(U32).indirect(list1[:]))
+        xs_g = shared.tile([P, J], U8, name="xs_g", align_bytes=64, offset=4 * J)
+        nc.vector.tensor_copy(xs_g[:], xs[:].indirect(list1[:]))
 
         planes = keep.tile([P, 2, PACK, HALF], BF16, name="planes", tag="step_then_planes", align_bytes=64)
         for j in range(PACK):
@@ -103,29 +104,39 @@ def tile_picked_tokens_codepage_one_grouptriple_one_plain_kernel(
             src = planes[:, h].rearrange("p j (m t) -> p t m j", t=PACK)
             nc.vector.tensor_copy(grouped[t][:, h * 64 : (h + 1) * 64, :], src[:, t])
 
-        for t in range(PACK):
-            interleave(0, t)
-        banks = []
-        interleave(1, 0)
-        for t in range(PACK):
-            if t + 1 < PACK:
-                interleave(1, t + 1)
+        hidden = [keep.tile([P, J], F32, name="hidden%d" % t) for t in range(PACK)]
+
+        def multiply(t):
             codes = keep.tile([P, P], U32, name="codes%d" % t, align_bytes=64)
             scales = keep.tile([P, P], U8, name="scales%d" % t, align_bytes=64)
             nc.vector.quantize_mx(
                 out=codes[:].bitcast(FP8X4), scales=scales[:], in_=grouped[t][:].rearrange("p m j -> p (m j)")
             )
-            bank = psum.tile([P, J], F32, name="hidden_bank%d" % t)
-            nc.tensor.matmul_mx(
-                out=bank[:], lhsT=codes[:].bitcast(FP8X4), lhsT_scale=scales[:],
-                rhs=xw_g[:].bitcast(FP8X4), rhs_scale=xs_g[:], start=True, stop=True,
-            )
-            banks.append(bank)
+            width = J // 2 if t == 0 else J
+            banks = []
+            for c0 in range(0, J, width):
+                cols = slice(c0, c0 + width)
+                bank = psum.tile([P, width], F32, name="hidden_bank%d_%d" % (t, c0), tag="bank%d_%d" % (t, c0))
+                nc.tensor.matmul_mx(
+                    out=bank[:], lhsT=codes[:].bitcast(FP8X4), lhsT_scale=scales[:],
+                    rhs=xw_g[:, cols].bitcast(FP8X4), rhs_scale=xs_g[:, cols], start=True, stop=True,
+                )
+                banks.append(bank)
+            return banks
 
-        hidden = [keep.tile([P, J], F32, name="hidden%d" % t) for t in range(PACK)]
-        nc.scalar.copy(hidden[0][:], banks[0][:])
+        for h in range(2):
+            interleave(h, 0)
+            interleave(h, 1)
+        for t in range(2, PACK):
+            nc.scalar.copy(
+                grouped[t][:].rearrange("p (h m) j -> p h m j", h=2),
+                planes[:].rearrange("p h j (m t) -> p t h m j", t=PACK)[:, t],
+            )
+        banks = [multiply(t) for t in range(PACK)]
+        nc.vector.tensor_copy(hidden[0][:, : J // 2], banks[0][0][:])
+        nc.scalar.copy(hidden[0][:, J // 2 :], banks[0][1][:])
         for t in range(1, PACK):
-            nc.vector.tensor_copy(hidden[t][:], banks[t][:])
+            nc.vector.tensor_copy(hidden[t][:], banks[t][0][:])
 
         total = keep.tile([P, PACK, O], F32, name="total")
         for t in range(PACK):

@@ -18,7 +18,12 @@ MAX = mybir.AluOpType.max
 
 P = 128
 PACK = 4
-HALF = R // 2
+QUADRANT = 32
+GROUP = 16
+R_HALF = R // 2
+M_HALF = P // 2
+J_HALF = J // 2
+ON_VECTOR = 2
 
 
 def tile_picked_tokens_codepage_one_grouptriple_one_plain_kernel(
@@ -37,136 +42,125 @@ def tile_picked_tokens_codepage_one_grouptriple_one_plain_kernel(
             nc.sync.dma_start(tile[:], src)
             return tile
 
-        def load_column(src, name, queue, tag):
+        def load_factors(src, name, queue, tag):
             tile = keep.tile([P, PACK], F32, name=name, tag=tag, align_bytes=64)
             queue.dma_start(tile[:], src.rearrange("(p t) o -> p (t o)", t=PACK))
             return tile
 
-        def load_scale_rows(plane, src):
-            for i in range(4):
-                nc.sync.dma_start(plane[i:P:32, :].bitcast(I32), src[0, i:16:4, :].bitcast(I32))
+        def load_words(src, name):
+            tile = keep.tile([P, src.shape[2]], I32, name=name, align_bytes=64)
+            nc.sync.dma_start(tile[:], src[0].rearrange("p c b -> p (c b)").bitcast(I32))
+            return tile
+
+        def load_scale_rows(tile, src):
+            for i in range(PACK):
+                nc.sync.dma_start(tile[i:P:QUADRANT, :].bitcast(I32), src[0, i :: PACK, :].bitcast(I32))
 
         warm = keep.tile([P, 2], F32, name="warm")
         nc.vector.memset(warm[:, 0:1], 0.0)
         nc.scalar.activation(warm[:, 1:2], warm[:, 0:1], COPY)
 
-        xs = keep.tile([P, T], U8, name="xs", align_bytes=64)
-        nc.vector.memset(xs[:].bitcast(I32), 0)
-        wbs = keep.tile([P, N], U8, name="wbs", align_bytes=64)
-        nc.vector.memset(wbs[:].bitcast(I32), 0)
+        xt_scale_tile = keep.tile([P, T], U8, name="xt_scale_tile", align_bytes=64)
+        nc.vector.memset(xt_scale_tile[:].bitcast(I32), 0)
+        wb_scale_tile = keep.tile([P, N], U8, name="wb_scale_tile", align_bytes=64)
+        nc.vector.memset(wb_scale_tile[:].bitcast(I32), 0)
         page = [keep.tile([P, G], F32, name="page%d" % t) for t in range(PACK)]
         for t in range(PACK):
             nc.vector.memset(page[t][:], 0.0)
 
         ua_rows = ua.rearrange("(p t) f -> p t f", t=PACK)
         table = [keep.tile([P, F], F32, name="table%d" % t) for t in range(PACK)]
-
-        list2 = load_list(offs2, "list2")
-        step = load_column(ha, "step", nc.scalar, "step_then_planes")
         nc.sync.dma_start(table[0][:], ua_rows[:, 0, :])
+        list2 = load_list(offs2, "list2")
+        step = load_factors(ha, "step", nc.scalar, "step_then_wc")
         list3 = load_list(offs3, "list3")
         for t in range(1, PACK - 1):
             nc.sync.dma_start(table[t][:], ua_rows[:, t, :])
         list1 = load_list(offs, "list1")
-        xw = keep.tile([P, T], I32, name="xw", align_bytes=64)
-        nc.sync.dma_start(xw[:], xt_words[0].rearrange("p c b -> p (c b)").bitcast(I32))
-        load_scale_rows(xs, xt_scales)
+        xt_word_tile = load_words(xt_words, "xt_word_tile")
+        load_scale_rows(xt_scale_tile, xt_scales)
         nc.sync.dma_start(table[PACK - 1][:], ua_rows[:, PACK - 1, :])
         list4 = load_list(offs4, "list4")
-        reading = load_column(hb, "reading", nc.sync, "reading")
+        reading = load_factors(hb, "reading", nc.sync, "reading")
         slot_lists = [load_list(src, "list%d" % (5 + i)) for i, src in enumerate((offs5, offs6, offs7))]
-        weights = [load_column(src, "weight%d" % i, nc.sync, "weight%d" % i) for i, src in enumerate((sa, sb, sd))]
-        wbw = keep.tile([P, N], I32, name="wbw", align_bytes=64)
-        nc.sync.dma_start(wbw[:], wb_words[0].rearrange("p c b -> p (c b)").bitcast(I32))
-        load_scale_rows(wbs, wb_scales)
+        weights = [load_factors(src, "weight%d" % i, nc.sync, "weight%d" % i) for i, src in enumerate((sa, sb, sd))]
+        wb_word_tile = load_words(wb_words, "wb_word_tile")
+        load_scale_rows(wb_scale_tile, wb_scales)
 
         for t in range(PACK):
             wcd = shared.tile([P, R], F32, name="wcd%d" % t, align_bytes=64, offset=4 * R * (PACK - 1 - t))
             nc.scalar.activation(wcd[:], table[t][:].indirect(list2[:]), COPY, scale=step[:, t : t + 1])
             nc.vector.tensor_copy(page[t][:].indirect(list3[:]), wcd[:])
 
-        xw_g = shared.tile([P, J], U32, name="xw_g", align_bytes=64, offset=0)
-        nc.vector.tensor_copy(xw_g[:], xw[:].bitcast(U32).indirect(list1[:]))
-        xs_g = shared.tile([P, J], U8, name="xs_g", align_bytes=64, offset=4 * J)
-        nc.vector.tensor_copy(xs_g[:], xs[:].indirect(list1[:]))
+        x_words = shared.tile([P, J], U32, name="x_words", align_bytes=64, offset=0)
+        nc.vector.tensor_copy(x_words[:], xt_word_tile[:].bitcast(U32).indirect(list1[:]))
+        x_scales = shared.tile([P, J], U8, name="x_scales", align_bytes=64, offset=4 * J)
+        nc.vector.tensor_copy(x_scales[:], xt_scale_tile[:].indirect(list1[:]))
 
-        planes = keep.tile([P, 2, PACK, HALF], BF16, name="planes", tag="step_then_planes", align_bytes=64)
+        wc = keep.tile([P, 2, PACK, R_HALF], BF16, name="wc", tag="step_then_wc", align_bytes=64)
         for j in range(PACK):
             for h in range(2):
-                cols = slice(h * HALF // 16, (h + 1) * HALF // 16)
-                nc.scalar.activation(
-                    planes[:, h, j, :], page[j][:].indirect(list4[:, cols]), COPY, scale=reading[:, j : j + 1]
-                )
+                entries = list4[:, h * R_HALF // GROUP : (h + 1) * R_HALF // GROUP]
+                nc.scalar.activation(wc[:, h, j, :], page[j][:].indirect(entries), COPY, scale=reading[:, j : j + 1])
 
         grouped = [keep.tile([P, P, PACK], BF16, name="grouped%d" % t, align_bytes=64) for t in range(PACK)]
-
-        def interleave(h, t):
-            src = planes[:, h].rearrange("p j (m t) -> p t m j", t=PACK)
-            nc.vector.tensor_copy(grouped[t][:, h * 64 : (h + 1) * 64, :], src[:, t])
-
         hidden = [keep.tile([P, J], F32, name="hidden%d" % t) for t in range(PACK)]
+        dealt = wc[:].rearrange("p h j (m t) -> p t h m j", t=PACK)
 
-        def multiply(t):
+        def multiply(t, width):
             codes = keep.tile([P, P], U32, name="codes%d" % t, align_bytes=64)
             scales = keep.tile([P, P], U8, name="scales%d" % t, align_bytes=64)
             nc.vector.quantize_mx(
                 out=codes[:].bitcast(FP8X4), scales=scales[:], in_=grouped[t][:].rearrange("p m j -> p (m j)")
             )
-            width = J // 2 if t == 0 else J
             banks = []
             for c0 in range(0, J, width):
                 cols = slice(c0, c0 + width)
-                bank = psum.tile([P, width], F32, name="hidden_bank%d_%d" % (t, c0), tag="bank%d_%d" % (t, c0))
+                bank = psum.tile([P, width], F32, name="hidden_bank%d_%d" % (t, c0))
                 nc.tensor.matmul_mx(
                     out=bank[:], lhsT=codes[:].bitcast(FP8X4), lhsT_scale=scales[:],
-                    rhs=xw_g[:, cols].bitcast(FP8X4), rhs_scale=xs_g[:, cols], start=True, stop=True,
+                    rhs=x_words[:, cols].bitcast(FP8X4), rhs_scale=x_scales[:, cols], start=True, stop=True,
                 )
                 banks.append(bank)
             return banks
 
         for h in range(2):
-            interleave(h, 0)
-            interleave(h, 1)
-        for t in range(2, PACK):
-            nc.scalar.copy(
-                grouped[t][:].rearrange("p (h m) j -> p h m j", h=2),
-                planes[:].rearrange("p h j (m t) -> p t h m j", t=PACK)[:, t],
-            )
-        banks = [multiply(t) for t in range(PACK)]
-        nc.vector.tensor_copy(hidden[0][:, : J // 2], banks[0][0][:])
-        nc.scalar.copy(hidden[0][:, J // 2 :], banks[0][1][:])
+            for t in range(ON_VECTOR):
+                nc.vector.tensor_copy(grouped[t][:, h * M_HALF : (h + 1) * M_HALF, :], dealt[:, t, h])
+        for t in range(ON_VECTOR, PACK):
+            nc.scalar.copy(grouped[t][:].rearrange("p (h m) j -> p h m j", h=2), dealt[:, t])
+        first_banks = multiply(0, J_HALF)
+        later_banks = [multiply(t, J)[0] for t in range(1, PACK)]
+        nc.vector.tensor_copy(hidden[0][:, :J_HALF], first_banks[0][:])
+        nc.scalar.copy(hidden[0][:, J_HALF:], first_banks[1][:])
         for t in range(1, PACK):
-            nc.vector.tensor_copy(hidden[t][:], banks[t][0][:])
-
-        total = keep.tile([P, PACK, O], F32, name="total")
-        for t in range(PACK):
-            terms = [keep.tile([P, O], F32, name="term%d_%d" % (t, i)) for i in range(3)]
-            for i in range(3):
-                nc.scalar.activation(
-                    terms[i][:], hidden[t][:].indirect(slot_lists[i][:]), COPY, scale=weights[i][:, t : t + 1]
-                )
-            pair = keep.tile([P, O], F32, name="pair%d" % t)
-            nc.vector.tensor_tensor(pair[:], terms[0][:], terms[1][:], ADD)
-            nc.vector.tensor_tensor(total[:, t, :], pair[:], terms[2][:], ADD)
+            nc.vector.tensor_copy(hidden[t][:], later_banks[t - 1][:])
 
         hid = keep.tile([P, O, PACK], BF16, name="hid", align_bytes=64)
-        nc.vector.tensor_scalar(hid[:], total[:].rearrange("p t o -> p o t"), 0.0, None, MAX)
+        for t in range(PACK):
+            terms = [keep.tile([P, O], F32, name="term%d_%d" % (t, i)) for i in range(len(slot_lists))]
+            for term, slots, weight in zip(terms, slot_lists, weights):
+                nc.scalar.activation(term[:], hidden[t][:].indirect(slots[:]), COPY, scale=weight[:, t : t + 1])
+            pair = keep.tile([P, O], F32, name="pair%d" % t)
+            nc.vector.tensor_tensor(pair[:], terms[0][:], terms[1][:], ADD)
+            total = keep.tile([P, O], F32, name="total%d" % t)
+            nc.vector.tensor_tensor(total[:], pair[:], terms[2][:], ADD)
+            nc.vector.tensor_scalar(hid[:, :, t], total[:], 0.0, None, MAX)
+
         hid_codes = keep.tile([P, O], U32, name="hid_codes", align_bytes=64)
         hid_scales = keep.tile([P, O], U8, name="hid_scales", align_bytes=64)
         nc.vector.quantize_mx(
             out=hid_codes[:].bitcast(FP8X4), scales=hid_scales[:], in_=hid[:].rearrange("p o t -> p (o t)")
         )
-        for h in range(N // P):
-            cols = slice(h * P, (h + 1) * P)
-            bank = psum.tile([P, O], F32, name="out_bank%d" % h)
+
+        ways_out = ((nc.scalar.copy, nc.scalar), (nc.vector.tensor_copy, nc.sync))
+        for b, (copy_out, queue) in enumerate(ways_out):
+            rows = slice(b * P, (b + 1) * P)
+            bank = psum.tile([P, O], F32, name="out_bank%d" % b)
             nc.tensor.matmul_mx(
-                out=bank[:], lhsT=wbw[:, cols].bitcast(FP8X4), lhsT_scale=wbs[:, cols],
+                out=bank[:], lhsT=wb_word_tile[:, rows].bitcast(FP8X4), lhsT_scale=wb_scale_tile[:, rows],
                 rhs=hid_codes[:].bitcast(FP8X4), rhs_scale=hid_scales[:], start=True, stop=True,
             )
-            result = keep.tile([P, O], F32, name="result%d" % h)
-            if h == 0:
-                nc.scalar.copy(result[:], bank[:])
-                nc.scalar.dma_start(out[cols, :], result[:])
-            else:
-                nc.vector.tensor_copy(result[:], bank[:])
-                nc.sync.dma_start(out[cols, :], result[:])
+            result = keep.tile([P, O], F32, name="result%d" % b)
+            copy_out(result[:], bank[:])
+            queue.dma_start(out[rows, :], result[:])

from contextlib import ExitStack

import concourse.mybir as mybir

K, J, R, T, F, G, O, N = 512, 256, 512, 512, 2048, 1024, 128, 256
FLOPS = 2 * K * R * J + 2 * R * N * O

F32 = mybir.dt.float32
BF16 = mybir.dt.bfloat16
I32 = mybir.dt.int32
U32 = mybir.dt.uint32
U16 = mybir.dt.uint16
U8 = mybir.dt.uint8
FP8X4 = mybir.dt.float8_e4m3fn_x4
COPY = mybir.ActivationFunctionType.Copy
ADD = mybir.AluOpType.add
MAX = mybir.AluOpType.max

P = 128
PACK = 4
QUADRANT = 32
GROUP = 16
R_HALF = R // 2
M_HALF = P // 2
J_HALF = J // 2
ON_VECTOR = 2


def tile_picked_tokens_codepage_one_grouptriple_one_plain_kernel(
    tc, xt_words, xt_scales, ua, ha, hb, sa, sb, sd, wb_words, wb_scales,
    offs, offs2, offs3, offs4, offs5, offs6, offs7, out,
):
    nc = tc.nc
    with ExitStack() as ctx:
        lists = ctx.enter_context(tc.tile_pool(name="lists", bufs=1))
        keep = ctx.enter_context(tc.tile_pool(name="keep", bufs=1))
        shared = ctx.enter_context(tc.tile_pool(name="shared", bufs=1))
        psum = ctx.enter_context(tc.psum_pool(name="psum", bufs=1))

        def load_list(src, name):
            tile = lists.tile(list(src.shape), U16, name=name)
            nc.sync.dma_start(tile[:], src)
            return tile

        def load_factors(src, name, queue, tag):
            tile = keep.tile([P, PACK], F32, name=name, tag=tag, align_bytes=64)
            queue.dma_start(tile[:], src.rearrange("(p t) o -> p (t o)", t=PACK))
            return tile

        def load_words(src, name):
            tile = keep.tile([P, src.shape[2]], I32, name=name, align_bytes=64)
            nc.sync.dma_start(tile[:], src[0].rearrange("p c b -> p (c b)").bitcast(I32))
            return tile

        def load_scale_rows(tile, src):
            for i in range(PACK):
                nc.sync.dma_start(tile[i:P:QUADRANT, :].bitcast(I32), src[0, i :: PACK, :].bitcast(I32))

        warm = keep.tile([P, 2], F32, name="warm")
        nc.vector.memset(warm[:, 0:1], 0.0)
        nc.scalar.activation(warm[:, 1:2], warm[:, 0:1], COPY)

        xt_scale_tile = keep.tile([P, T], U8, name="xt_scale_tile", align_bytes=64)
        nc.vector.memset(xt_scale_tile[:].bitcast(I32), 0)
        wb_scale_tile = keep.tile([P, N], U8, name="wb_scale_tile", align_bytes=64)
        nc.vector.memset(wb_scale_tile[:].bitcast(I32), 0)
        page = [keep.tile([P, G], F32, name="page%d" % t) for t in range(PACK)]
        for t in range(PACK):
            nc.vector.memset(page[t][:], 0.0)

        ua_rows = ua.rearrange("(p t) f -> p t f", t=PACK)
        table = [keep.tile([P, F], F32, name="table%d" % t) for t in range(PACK)]
        nc.sync.dma_start(table[0][:], ua_rows[:, 0, :])
        list2 = load_list(offs2, "list2")
        step = load_factors(ha, "step", nc.scalar, "step_then_wc")
        list3 = load_list(offs3, "list3")
        for t in range(1, PACK - 1):
            nc.sync.dma_start(table[t][:], ua_rows[:, t, :])
        list1 = load_list(offs, "list1")
        xt_word_tile = load_words(xt_words, "xt_word_tile")
        load_scale_rows(xt_scale_tile, xt_scales)
        nc.sync.dma_start(table[PACK - 1][:], ua_rows[:, PACK - 1, :])
        list4 = load_list(offs4, "list4")
        reading = load_factors(hb, "reading", nc.sync, "reading")
        slot_lists = [load_list(src, "list%d" % (5 + i)) for i, src in enumerate((offs5, offs6, offs7))]
        weights = [load_factors(src, "weight%d" % i, nc.sync, "weight%d" % i) for i, src in enumerate((sa, sb, sd))]
        wb_word_tile = load_words(wb_words, "wb_word_tile")
        load_scale_rows(wb_scale_tile, wb_scales)

        for t in range(PACK):
            wcd = shared.tile([P, R], F32, name="wcd%d" % t, align_bytes=64, offset=4 * R * (PACK - 1 - t))
            nc.scalar.activation(wcd[:], table[t][:].indirect(list2[:]), COPY, scale=step[:, t : t + 1])
            nc.vector.tensor_copy(page[t][:].indirect(list3[:]), wcd[:])

        x_words = shared.tile([P, J], U32, name="x_words", align_bytes=64, offset=0)
        nc.vector.tensor_copy(x_words[:], xt_word_tile[:].bitcast(U32).indirect(list1[:]))
        x_scales = shared.tile([P, J], U8, name="x_scales", align_bytes=64, offset=4 * J)
        nc.vector.tensor_copy(x_scales[:], xt_scale_tile[:].indirect(list1[:]))

        wc = keep.tile([P, 2, PACK, R_HALF], BF16, name="wc", tag="step_then_wc", align_bytes=64)
        for j in range(PACK):
            for h in range(2):
                entries = list4[:, h * R_HALF // GROUP : (h + 1) * R_HALF // GROUP]
                nc.scalar.activation(wc[:, h, j, :], page[j][:].indirect(entries), COPY, scale=reading[:, j : j + 1])

        grouped = [keep.tile([P, P, PACK], BF16, name="grouped%d" % t, align_bytes=64) for t in range(PACK)]
        hidden = [keep.tile([P, J], F32, name="hidden%d" % t) for t in range(PACK)]
        dealt = wc[:].rearrange("p h j (m t) -> p t h m j", t=PACK)

        def multiply(t, width):
            codes = keep.tile([P, P], U32, name="codes%d" % t, align_bytes=64)
            scales = keep.tile([P, P], U8, name="scales%d" % t, align_bytes=64)
            nc.vector.quantize_mx(
                out=codes[:].bitcast(FP8X4), scales=scales[:], in_=grouped[t][:].rearrange("p m j -> p (m j)")
            )
            banks = []
            for c0 in range(0, J, width):
                cols = slice(c0, c0 + width)
                bank = psum.tile([P, width], F32, name="hidden_bank%d_%d" % (t, c0))
                nc.tensor.matmul_mx(
                    out=bank[:], lhsT=codes[:].bitcast(FP8X4), lhsT_scale=scales[:],
                    rhs=x_words[:, cols].bitcast(FP8X4), rhs_scale=x_scales[:, cols], start=True, stop=True,
                )
                banks.append(bank)
            return banks

        for h in range(2):
            for t in range(ON_VECTOR):
                nc.vector.tensor_copy(grouped[t][:, h * M_HALF : (h + 1) * M_HALF, :], dealt[:, t, h])
        for t in range(ON_VECTOR, PACK):
            nc.scalar.copy(grouped[t][:].rearrange("p (h m) j -> p h m j", h=2), dealt[:, t])
        first_banks = multiply(0, J_HALF)
        later_banks = [multiply(t, J)[0] for t in range(1, PACK)]
        nc.vector.tensor_copy(hidden[0][:, :J_HALF], first_banks[0][:])
        nc.scalar.copy(hidden[0][:, J_HALF:], first_banks[1][:])
        for t in range(1, PACK):
            nc.vector.tensor_copy(hidden[t][:], later_banks[t - 1][:])

        hid = keep.tile([P, O, PACK], BF16, name="hid", align_bytes=64)
        for t in range(PACK):
            terms = [keep.tile([P, O], F32, name="term%d_%d" % (t, i)) for i in range(len(slot_lists))]
            for term, slots, weight in zip(terms, slot_lists, weights):
                nc.scalar.activation(term[:], hidden[t][:].indirect(slots[:]), COPY, scale=weight[:, t : t + 1])
            pair = keep.tile([P, O], F32, name="pair%d" % t)
            nc.vector.tensor_tensor(pair[:], terms[0][:], terms[1][:], ADD)
            total = keep.tile([P, O], F32, name="total%d" % t)
            nc.vector.tensor_tensor(total[:], pair[:], terms[2][:], ADD)
            nc.vector.tensor_scalar(hid[:, :, t], total[:], 0.0, None, MAX)

        hid_codes = keep.tile([P, O], U32, name="hid_codes", align_bytes=64)
        hid_scales = keep.tile([P, O], U8, name="hid_scales", align_bytes=64)
        nc.vector.quantize_mx(
            out=hid_codes[:].bitcast(FP8X4), scales=hid_scales[:], in_=hid[:].rearrange("p o t -> p (o t)")
        )

        ways_out = ((nc.scalar.copy, nc.scalar), (nc.vector.tensor_copy, nc.sync))
        for b, (copy_out, queue) in enumerate(ways_out):
            rows = slice(b * P, (b + 1) * P)
            bank = psum.tile([P, O], F32, name="out_bank%d" % b)
            nc.tensor.matmul_mx(
                out=bank[:], lhsT=wb_word_tile[:, rows].bitcast(FP8X4), lhsT_scale=wb_scale_tile[:, rows],
                rhs=hid_codes[:].bitcast(FP8X4), rhs_scale=hid_scales[:], start=True, stop=True,
            )
            result = keep.tile([P, O], F32, name="result%d" % b)
            copy_out(result[:], bank[:])
            queue.dma_start(out[rows, :], result[:])
